import numpy as np
import ml_dtypes


def mxq(x, axis, fmt="e4m3"):
    dtype, down = {"e4m3": (ml_dtypes.float8_e4m3fn, 7), "e5m2": (ml_dtypes.float8_e5m2, 14)}[fmt]
    v = np.moveaxis(np.asarray(x, np.float32).astype(ml_dtypes.bfloat16).astype(np.float64), axis, -1)
    blocks = v.reshape(v.shape[:-1] + (-1, 32))
    amax = np.abs(blocks).max(-1, keepdims=True)
    byte = np.maximum(np.where(amax > 0, np.frexp(amax)[1] - 1 + 127, 0) - down, 1)
    scale = np.exp2(byte - 127.0)
    codes = (blocks / scale).astype(np.float32).astype(dtype).astype(np.float64)
    return np.moveaxis((codes * scale).reshape(v.shape), -1, axis)


WIDE = False


def mx_kscale(k):
    if not WIDE:
        return np.ones(k)
    levels = np.array([10, -10, 5, -5, 0])
    if k % 512:
        return np.exp2(np.random.permutation(np.resize(levels, k // 32))).repeat(32)
    a = np.empty((k // 512, 16))
    for p in range(k // 512):
        a[p, :8] = np.random.permutation(np.resize(levels, 8))
        for g in range(8):
            far = levels[np.abs(levels - a[p, g]) >= 10]
            a[p, g + 8] = far[np.random.randint(len(far))]
    return np.exp2(a.ravel()).repeat(32)


def f64(x):
    return np.asarray(x).astype(np.float64)


def striped(idx):
    return np.tile(idx.reshape(-1, 16).T, (8, 1)).astype(np.uint16)


def unstriped(offs):
    return offs[:16].T.reshape(-1).astype(np.int64)


E2M1 = np.array([0.0, 0.5, 1.0, 1.5, 2.0, 3.0, 4.0, 6.0, -0.0, -0.5, -1.0, -1.5, -2.0, -3.0, -4.0, -6.0])


def pack_weight(w, fmt):
    k, n = w.shape
    w = f64(np.asarray(w, np.float32).astype(ml_dtypes.bfloat16)).reshape(k // 32, 32, n)
    amax = np.abs(w).max(1)
    if fmt == "e4m3":
        byte = np.frexp(amax)[1] - 1 + 127 - 7
    else:
        mant, ex = np.frexp(amax / 6.0)
        byte = np.where(mant > 0.5, ex, ex - 1) + 127
    byte = np.clip(np.where(amax > 0, byte, 1), 1, 254)
    scaled = (w * np.exp2(127.0 - byte)[:, None, :]).reshape(k, n).astype(np.float32)
    by_word = np.ascontiguousarray(scaled.reshape(k // 512, 128, 4, n).transpose(0, 1, 3, 2))
    if fmt == "e4m3":
        words = by_word.astype(ml_dtypes.float8_e4m3fn).view(np.uint8)
    else:
        c = by_word.astype(ml_dtypes.float4_e2m1fn).view(np.uint8) & 0xF
        words = (c[..., 0::2] | (c[..., 1::2] << 4)).reshape(k // 512, 128, 2 * n)
    return np.ascontiguousarray(words), np.ascontiguousarray(byte.astype(np.uint8).reshape(k // 512, 16, n))


def unpack_weight(words, scales, fmt):
    g, _, n = scales.shape
    words = np.ascontiguousarray(words).reshape(g, 128, n, -1)
    if fmt == "e4m3":
        vals = words.view(ml_dtypes.float8_e4m3fn).astype(np.float64)
    else:
        nib = np.empty((g, 128, n, 4), np.uint8)
        nib[..., 0::2] = words & 0xF
        nib[..., 1::2] = words >> 4
        vals = E2M1[nib]
    vals = vals * np.repeat(np.exp2(scales.astype(np.float64) - 127.0), 8, axis=1)[..., None]
    return vals.transpose(0, 1, 3, 2).reshape(g * 512, n)


def relu(v):
    return np.maximum(v, 0.0)


K, T, E, C, H, N = 1536, 768, 4, 256, 512, 128
PAD = 32


def by_expert(wq, xq):
    return np.concatenate([wq[e].T @ xq[:, e * C:(e + 1) * C] for e in range(E)], axis=1)


def setup_inputs():
    n = np.random.standard_normal
    s = mx_kscale(K)[:, None]
    u = mx_kscale(H)
    first = np.random.permutation(np.repeat(np.arange(E), T // E))
    second = (first + 1 + np.random.permutation(np.repeat(np.arange(E - 1), -(-T // (E - 1)))[:T])) % E
    while np.bincount(second, minlength=E).max() != T // E:
        load = np.bincount(second, minlength=E); hi, lo = int(load.argmax()), int(load.argmin())
        t = np.flatnonzero((second == hi) & (first != lo))[0]; second[t] = lo
    slot_token = np.empty(E * C, np.int64); pos = np.empty((2, T), np.int64); fill = np.zeros(E, np.int64)
    place = np.stack([np.random.permutation(C) for _ in range(E)])
    for r, deal in enumerate((first, second)):
        for t in np.random.permutation(T):
            e = deal[t]
            if fill[e] < C: j = e * C + place[e, fill[e]]; fill[e] += 1; slot_token[j] = t; pos[r, t] = j
            else: pos[r, t] = E * C + t % PAD
    g = np.random.uniform(0.2, 0.8, T)
    w1 = [pack_weight(m, "e2m1") for m in n((E, K, H)) / np.sqrt(K) / s[None]]
    w3 = [pack_weight(m, "e2m1") for m in n((E, K, H)) / np.sqrt(K) / s[None] * u[None, None, :]]
    w2 = [pack_weight(m, "e2m1") for m in n((E, H, N)) / np.sqrt(H) / u[None, :, None]]
    return {
        "xT": (n((K, T)) * s).astype(np.float32),
        "w1_words": np.stack([m[0] for m in w1]),
        "w1_scales": np.stack([m[1] for m in w1]),
        "w3_words": np.stack([m[0] for m in w3]),
        "w3_scales": np.stack([m[1] for m in w3]),
        "w2_words": np.stack([m[0] for m in w2]),
        "w2_scales": np.stack([m[1] for m in w2]),
        "gate": np.stack([np.tile(g, (N, 1)), np.tile(1.0 - g, (N, 1))]).astype(np.float32),
        "offs": striped(slot_token),
        "pos1": striped(pos[0]),
        "pos2": striped(pos[1]),
    }


def reference(xT, w1_words, w1_scales, w3_words, w3_scales, w2_words, w2_scales, gate, offs, pos1, pos2):
    idx = unstriped(offs)
    w1 = np.stack([unpack_weight(w1_words[e], w1_scales[e], "e2m1") for e in range(E)])
    w3 = np.stack([unpack_weight(w3_words[e], w3_scales[e], "e2m1") for e in range(E)])
    w2 = np.stack([unpack_weight(w2_words[e], w2_scales[e], "e2m1") for e in range(E)])
    xq = mxq(f64(xT)[:, idx], 0, "e4m3")
    h = relu(by_expert(w1, xq))
    h = h * by_expert(w3, xq)
    y = by_expert(w2, mxq(h, 0, "e4m3"))
    y = np.concatenate([y, np.zeros((N, PAD))], axis=1)
    return f64(gate[0]) * y[:, unstriped(pos1)] + f64(gate[1]) * y[:, unstriped(pos2)]

@@ -1,0 +1,229 @@
+from contextlib import ExitStack
+
+import concourse.mybir as mybir
+from concourse.masks import make_identity
+
+K, T, E, C, H, N = 1536, 768, 4, 256, 512, 128
+PAD = 32
+FLOPS = 3355443200
+
+F32 = mybir.dt.float32
+BF16 = mybir.dt.bfloat16
+U32 = mybir.dt.uint32
+I32 = mybir.dt.int32
+U16 = mybir.dt.uint16
+U8 = mybir.dt.uint8
+FP8X4 = mybir.dt.float8_e4m3fn_x4
+FP4X4 = mybir.dt.float4_e2m1fn_x4
+COPY = mybir.ActivationFunctionType.Copy
+RELU = mybir.ActivationFunctionType.Relu
+MULT = mybir.AluOpType.mult
+ADD = mybir.AluOpType.add
+
+P = 128
+PASSES = K // 512
+SLOTS = E * C
+CHUNK = 256
+VECTOR_CHUNKS = {(0, 0), (0, 2)}
+BANKS = ((0, 1), (2, 3), (4, 5), (6, 7), (1, 3), (5, 7), (0, 2), (4, 6))
+PIECE = {"A": (0, 256), "B": (256, 512), "F": (0, 512), "C": (512, 1024)}
+
+
+def tile_moe_cap2_glu_relu_kernel(
+    tc, xT, w1_words, w1_scales, w3_words, w3_scales, w2_words, w2_scales, gate, offs, pos1, pos2, out
+):
+    nc = tc.nc
+    with ExitStack() as ctx:
+        keep = ctx.enter_context(tc.tile_pool(name="keep", bufs=1))
+        stage = ctx.enter_context(tc.tile_pool(name="stage", bufs=4))
+        psum = ctx.enter_context(tc.psum_pool(name="psum", bufs=1))
+
+        offs_t = keep.tile([P, SLOTS // 16], U16, name="offs_t")
+        pos1_t = keep.tile([P, T // 16], U16, name="pos1_t")
+        pos2_t = keep.tile([P, T // 16], U16, name="pos2_t")
+        xf = [keep.tile([P, 4, T], F32, name=f"xf{s}") for s in range(PASSES)]
+        xb = [keep.tile([P, 4 * T], BF16, name=f"xb{s}", align_bytes=64) for s in range(PASSES)]
+        xw = [keep.tile([P, T], U32, name=f"xw{s}", align_bytes=64) for s in range(PASSES)]
+        xs = [keep.tile([P, T], U8, name=f"xs{s}", align_bytes=64) for s in range(PASSES)]
+        gw = [keep.tile([P, SLOTS], U32, name=f"gw{s}", align_bytes=64) for s in range(PASSES)]
+        gs = [keep.tile([P, SLOTS], U8, name=f"gs{s}", align_bytes=64) for s in range(PASSES)]
+        w1 = [keep.tile([P, PASSES, 2 * H], U8, name=f"w1_{e}", align_bytes=64) for e in range(E)]
+        w3 = [keep.tile([P, PASSES, 2 * H], U8, name=f"w3_{e}", align_bytes=64) for e in range(E)]
+        w2 = keep.tile([P, E, 2 * N], U8, name="w2", align_bytes=64)
+        w1s = keep.tile([P, E * PASSES, H], U8, name="w1s", align_bytes=64)
+        w3s = keep.tile([P, E * PASSES, H], U8, name="w3s", align_bytes=64)
+        w2s = keep.tile([P, E, N], U8, name="w2s", align_bytes=64)
+        gates = keep.tile([P, 2, T], F32, name="gates")
+        y = keep.tile([P, SLOTS + PAD], F32, name="y")
+        ident = keep.tile([P, P], F32, name="ident")
+
+        def load_x(s):
+            rows = xT[512 * s : 512 * (s + 1), :].rearrange("(p j) t -> p j t", j=4)
+            for start, stop in ((0, 256), (256, 512), (512, 768)) if s == 0 else ((0, 512), (512, 768)):
+                cols = slice(start, stop)
+                nc.sync.dma_start(out=xf[s][:, :, cols], in_=rows[:, :, cols])
+
+        def load_w(e):
+            for tile, dram in ((w1[e], w1_words), (w3[e], w3_words)):
+                nc.sync.dma_start(out=tile[:].bitcast(I32), in_=dram[e].rearrange("s p n -> p s n").bitcast(I32))
+
+        def load_scales(queue, tile, dram):
+            rows = dram.rearrange("e s q n -> q (e s) n")
+            for quad in range(4):
+                queue.dma_start(
+                    out=tile[32 * quad : 32 * quad + 4, :, :].bitcast(I32),
+                    in_=rows[4 * quad : 4 * quad + 4, :, :].bitcast(I32),
+                )
+
+        for tile in (w3s, w1s, w2s):
+            nc.vector.memset(tile[:].bitcast(I32), 0)
+        for s in range(PASSES):
+            nc.vector.memset(xs[s][:].bitcast(I32), 0)
+        nc.gpsimd.memset(y[:, SLOTS:], 0.0)
+        make_identity(nc, ident[:])
+
+        load_x(0)
+        nc.sync.dma_start(offs_t[:], offs)
+        load_scales(nc.sync, w3s, w3_scales)
+        load_scales(nc.gpsimd, w1s, w1_scales)
+        load_x(1)
+        load_w(0)
+        load_x(2)
+        load_w(1)
+        load_w(2)
+        load_w(3)
+        load_scales(nc.gpsimd, w2s, w2_scales)
+        nc.sync.dma_start(out=w2[:].bitcast(I32), in_=w2_words[:, 0].rearrange("e p n -> p e n").bitcast(I32))
+        nc.sync.dma_start(pos1_t[:], pos1)
+        nc.sync.dma_start(pos2_t[:], pos2)
+        nc.sync.dma_start(out=gates[:], in_=gate.rearrange("r p t -> p r t"))
+
+        def prepare(s):
+            for c in range(3):
+                dst = xb[s][:, 4 * CHUNK * c : 4 * CHUNK * (c + 1)].rearrange("p (t j) -> p t j", j=4)
+                src = xf[s][:, :, CHUNK * c : CHUNK * (c + 1)].rearrange("p j t -> p t j")
+                if (s, c) in VECTOR_CHUNKS:
+                    nc.vector.tensor_copy(dst, src)
+                else:
+                    nc.scalar.activation(dst, src, COPY)
+            for start, stop in ((0, 512), (512, 768)):
+                cols = slice(start, stop)
+                nc.vector.quantize_mx(
+                    out=xw[s][:, cols].bitcast(FP8X4), scales=xs[s][:, cols], in_=xb[s][:, 4 * start : 4 * stop]
+                )
+
+        def g_words(s, piece):
+            start, stop = PIECE[piece]
+            nc.vector.tensor_copy(gw[s][:, start:stop], xw[s][:].indirect(offs_t[:, start // 16 : stop // 16]))
+
+        def g_bytes(s, piece):
+            start, stop = PIECE[piece]
+            nc.vector.tensor_copy(gs[s][:, start:stop], xs[s][:].indirect(offs_t[:, start // 16 : stop // 16]))
+
+        acc, act, hid, hbf, codes = {}, {}, {}, {}, {}
+
+        def open_banks(half):
+            acc[half] = [psum.tile([P, H], F32, name=f"bank{b}") for b in BANKS[half]]
+
+        def mm(half, s, which=(0, 1)):
+            if half not in acc:
+                open_banks(half)
+            e = half // 2
+            slots = slice(128 * half, 128 * (half + 1))
+            for m in which:
+                w, ws = ((w1, w1s), (w3, w3s))[m]
+                nc.tensor.matmul_mx(
+                    out=acc[half][m][:],
+                    lhsT=gw[s][:, slots].bitcast(FP8X4),
+                    lhsT_scale=gs[s][:, slots],
+                    rhs=w[e][:, s, :].bitcast(FP4X4),
+                    rhs_scale=ws[:, PASSES * e + s, :],
+                    start=(s == 0),
+                    stop=(s == PASSES - 1),
+                )
+
+        def relu(half):
+            act[half] = stage.tile([P, H], F32, name="ra")
+            nc.scalar.activation(
+                act[half][:].rearrange("m (u p d) -> m u p d", u=2, d=2),
+                acc[half][0][:].rearrange("m (p u d) -> m u p d", u=2, d=2),
+                RELU,
+            )
+
+        def mul(half):
+            hid[half] = stage.tile([P, H], BF16, name="h", align_bytes=64)
+            nc.vector.tensor_tensor(
+                hid[half][:].rearrange("m (u p d) -> m u p d", u=2, d=2),
+                acc[half][1][:].rearrange("m (p u d) -> m u p d", u=2, d=2),
+                act[half][:].rearrange("m (u p d) -> m u p d", u=2, d=2),
+                MULT,
+            )
+
+        def tr(half):
+            words = hid[half][:].bitcast(F32)
+            for u in range(2):
+                cols = slice(128 * u, 128 * (u + 1))
+                nc.tensor.transpose(acc[half][0][:, cols], words[:, cols], ident[:])
+
+        def tcp(half):
+            hbf[half] = stage.tile([P, 4 * 128], BF16, name="hb", align_bytes=64)
+            nc.scalar.copy(
+                hbf[half][:].bitcast(F32).rearrange("p (r u) -> p r u", u=2),
+                acc[half][0][:, 0:256].rearrange("p (u r) -> p r u", u=2),
+            )
+
+        def hq(half):
+            hw = stage.tile([P, 128], U32, name="hw", align_bytes=64)
+            hs = stage.tile([P, 128], U8, name="hs", align_bytes=64)
+            nc.vector.quantize_mx(out=hw[:].bitcast(FP8X4), scales=hs[:], in_=hbf[half][:])
+            codes[half] = (hw, hs)
+
+        def m2(half):
+            e = half // 2
+            hw, hs = codes[half]
+            nc.tensor.matmul_mx(
+                out=acc[half][0][:, 256:384],
+                lhsT=w2[:, e, :].bitcast(FP4X4),
+                lhsT_scale=w2s[:, e, :],
+                rhs=hw[:].bitcast(FP8X4),
+                rhs_scale=hs[:],
+                start=True,
+                stop=True,
+            )
+
+        def ycp(half):
+            nc.scalar.copy(y[:, 128 * half : 128 * (half + 1)], acc[half][0][:, 256:384])
+
+        prepare(0); g_words(0, "F"); g_bytes(0, "F")
+        for h in range(4):
+            mm(h, 0)
+        g_bytes(0, "C")
+        prepare(1); g_words(1, "F"); g_words(0, "C"); g_bytes(1, "F"); g_words(1, "C")
+        for h in range(4):
+            mm(h, 1)
+        prepare(2); g_bytes(2, "A"); g_words(2, "A"); g_words(2, "B"); g_bytes(2, "B")
+        for h in range(4):
+            mm(h, 2); relu(h)
+        mul(0); mul(1); g_bytes(1, "C"); mul(2); mul(3)
+        tr(0); tr(1); tcp(0); tcp(1); mm(4, 0); hq(0); hq(1)
+        mm(4, 1); m2(0); m2(1); ycp(0); ycp(1); mm(5, 0); mm(5, 1)
+        g_words(2, "C"); g_bytes(2, "C")
+        tr(2); tr(3); tcp(2); tcp(3); hq(2); hq(3)
+        m2(2); m2(3); ycp(2); ycp(3)
+        mm(6, 0); mm(4, 2); relu(4); mm(5, 2); relu(5); mm(6, 1); mm(6, 2); relu(6); mm(7, 0); mul(4); mul(5)
+        tr(4); tr(5); tcp(4); tcp(5); mm(7, 1); mm(7, 2, (0,)); relu(7); mm(7, 2, (1,)); mul(6); hq(4); hq(5); mul(7)
+        tr(6); m2(4); m2(5); tr(7); tcp(6); ycp(4); ycp(5); tcp(7); hq(6); hq(7); m2(6); ycp(6); m2(7); ycp(7)
+
+        parts = []
+        for c in range(2):
+            cols = slice(384 * c, 384 * (c + 1))
+            idx = slice(24 * c, 24 * (c + 1))
+            t1 = stage.tile([P, 384], F32, name="t1")
+            t2 = stage.tile([P, 384], F32, name="t2")
+            nc.vector.tensor_tensor(t1[:], y[:].indirect(pos1_t[:, idx]), gates[:, 0, cols], MULT)
+            nc.vector.tensor_tensor(t2[:], y[:].indirect(pos2_t[:, idx]), gates[:, 1, cols], MULT)
+            parts.append((cols, t1, t2))
+        for cols, t1, t2 in parts:
+            o = stage.tile([P, 384], F32, name="o")
+            nc.vector.tensor_tensor(o[:], t1[:], t2[:], ADD)
+            nc.sync.dma_start(out=out[:, cols], in_=o[:])

@@ -59,19 +59,18 @@ def tile_moe_cap2_glu_relu_kernel(
 
         def load_x(s):
             rows = xT[512 * s : 512 * (s + 1), :].rearrange("(p j) t -> p j t", j=4)
-            for start, stop in ((0, 256), (256, 512), (512, 768)) if s == 0 else ((0, 512), (512, 768)):
-                cols = slice(start, stop)
-                nc.sync.dma_start(out=xf[s][:, :, cols], in_=rows[:, :, cols])
+            nc.sync.dma_start(out=xf[s][:], in_=rows)
 
         def load_w(e):
             for tile, dram in ((w1[e], w1_words), (w3[e], w3_words)):
                 nc.sync.dma_start(out=tile[:].bitcast(I32), in_=dram[e].rearrange("s p n -> p s n").bitcast(I32))
 
-        def load_scales(queue, tile, dram):
-            rows = dram.rearrange("e s q n -> q (e s) n")
+        def load_scales(tile, dram, e0, e1):
+            passes = dram.shape[1]
+            rows = dram[e0:e1].rearrange("e s q n -> q (e s) n")
             for quad in range(4):
-                queue.dma_start(
-                    out=tile[32 * quad : 32 * quad + 4, :, :].bitcast(I32),
+                nc.sync.dma_start(
+                    out=tile[32 * quad : 32 * quad + 4, passes * e0 : passes * e1, :].bitcast(I32),
                     in_=rows[4 * quad : 4 * quad + 4, :, :].bitcast(I32),
                 )
 
@@ -84,15 +83,17 @@ def tile_moe_cap2_glu_relu_kernel(
 
         load_x(0)
         nc.sync.dma_start(offs_t[:], offs)
-        load_scales(nc.sync, w3s, w3_scales)
-        load_scales(nc.gpsimd, w1s, w1_scales)
         load_x(1)
-        load_w(0)
         load_x(2)
+        load_scales(w1s, w1_scales, 0, 2)
+        load_scales(w3s, w3_scales, 0, 2)
+        load_w(0)
         load_w(1)
         load_w(2)
+        load_scales(w1s, w1_scales, 2, 4)
+        load_scales(w3s, w3_scales, 2, 4)
         load_w(3)
-        load_scales(nc.gpsimd, w2s, w2_scales)
+        load_scales(w2s, w2_scales, 0, 4)
         nc.sync.dma_start(out=w2[:].bitcast(I32), in_=w2_words[:, 0].rearrange("e p n -> p e n").bitcast(I32))
         nc.sync.dma_start(pos1_t[:], pos1)
         nc.sync.dma_start(pos2_t[:], pos2)
@@ -100,8 +101,8 @@ def tile_moe_cap2_glu_relu_kernel(
 
         def prepare(s):
             for c in range(3):
-                dst = xb[s][:, 4 * CHUNK * c : 4 * CHUNK * (c + 1)].rearrange("p (t j) -> p t j", j=4)
-                src = xf[s][:, :, CHUNK * c : CHUNK * (c + 1)].rearrange("p j t -> p t j")
+                dst = xb[s][:, 4 * CHUNK * c : 4 * CHUNK * (c + 1)].rearrange("p (c i j) -> p c j i", i=4, j=4)
+                src = xf[s][:, :, CHUNK * c : CHUNK * (c + 1)].rearrange("p j (c i) -> p c j i", i=4)
                 if (s, c) in VECTOR_CHUNKS:
                     nc.vector.tensor_copy(dst, src)
                 else:
@@ -194,24 +195,25 @@ def tile_moe_cap2_glu_relu_kernel(
         def ycp(half):
             nc.scalar.copy(y[:, 128 * half : 128 * (half + 1)], acc[half][0][:, 256:384])
 
-        prepare(0); g_words(0, "F"); g_bytes(0, "F")
-        for h in range(4):
-            mm(h, 0)
-        g_bytes(0, "C")
-        prepare(1); g_words(1, "F"); g_words(0, "C"); g_bytes(1, "F"); g_words(1, "C")
-        for h in range(4):
-            mm(h, 1)
-        prepare(2); g_bytes(2, "A"); g_words(2, "A"); g_words(2, "B"); g_bytes(2, "B")
-        for h in range(4):
+        prepare(0); g_words(0, "F"); g_bytes(0, "F"); g_bytes(0, "C")
+        prepare(1); g_words(1, "F"); g_bytes(1, "F")
+        prepare(2); g_bytes(2, "A"); g_words(2, "A"); g_words(0, "C"); g_words(2, "B"); g_bytes(2, "B")
+        for h in (0, 1):
+            mm(h, 0); mm(h, 1)
+        for h in (0, 1):
             mm(h, 2); relu(h)
-        mul(0); mul(1); g_bytes(1, "C"); mul(2); mul(3)
+        for h in (2, 3):
+            mm(h, 0); mm(h, 1)
+        for h in (2, 3):
+            mm(h, 2); relu(h)
+        g_words(1, "C"); mul(0); mul(1); g_bytes(1, "C"); mul(2); mul(3)
         tr(0); tr(1); tcp(0); tcp(1); mm(4, 0); hq(0); hq(1)
-        mm(4, 1); m2(0); m2(1); ycp(0); ycp(1); mm(5, 0); mm(5, 1)
         g_words(2, "C"); g_bytes(2, "C")
-        tr(2); tr(3); tcp(2); tcp(3); hq(2); hq(3)
-        m2(2); m2(3); ycp(2); ycp(3)
-        mm(6, 0); mm(4, 2); relu(4); mm(5, 2); relu(5); mm(6, 1); mm(6, 2); relu(6); mm(7, 0); mul(4); mul(5)
-        tr(4); tr(5); tcp(4); tcp(5); mm(7, 1); mm(7, 2, (0,)); relu(7); mm(7, 2, (1,)); mul(6); hq(4); hq(5); mul(7)
+        mm(4, 1); tr(2); tr(3); tcp(2); tcp(3); m2(0); m2(1); ycp(0); ycp(1); mm(5, 0); mm(5, 1)
+        hq(2); hq(3)
+        m2(2); m2(3); ycp(2); ycp(3); mm(6, 0); mm(4, 2); relu(4); mm(5, 2); relu(5)
+        mm(6, 1); mm(6, 2); relu(6); mm(7, 0); mul(4); mul(5)
+        mm(7, 1); tr(4); tr(5); tcp(4); tcp(5); mm(7, 2, (0,)); relu(7); mm(7, 2, (1,)); mul(6); hq(4); hq(5); mul(7)
         tr(6); m2(4); m2(5); tr(7); tcp(6); ycp(4); ycp(5); tcp(7); hq(6); hq(7); m2(6); ycp(6); m2(7); ycp(7)
 
         parts = []

@@ -24,7 +24,7 @@ P = 128
 PASSES = K // 512
 SLOTS = E * C
 CHUNK = 256
-VECTOR_CHUNKS = {(0, 0), (0, 2)}
+VECTOR_CHUNKS = {(0, 0), (0, 2), (1, 1)}
 BANKS = ((0, 1), (2, 3), (4, 5), (6, 7), (1, 3), (5, 7), (0, 2), (4, 6))
 PIECE = {"A": (0, 256), "B": (256, 512), "F": (0, 512), "C": (512, 1024)}
 
@@ -44,7 +44,8 @@ def tile_moe_cap2_glu_relu_kernel(
         xf = [keep.tile([P, 4, T], F32, name=f"xf{s}") for s in range(PASSES)]
         xb = [keep.tile([P, 4 * T], BF16, name=f"xb{s}", align_bytes=64) for s in range(PASSES)]
         xw = [keep.tile([P, T], U32, name=f"xw{s}", align_bytes=64) for s in range(PASSES)]
-        xs = [keep.tile([P, T], U8, name=f"xs{s}", align_bytes=64) for s in range(PASSES)]
+        xs01 = keep.tile([P, T], U8, name="xs01", align_bytes=64)
+        xs2 = keep.tile([P, T], U8, name="xs2", align_bytes=64)
         gw = [keep.tile([P, SLOTS], U32, name=f"gw{s}", align_bytes=64) for s in range(PASSES)]
         gs = [keep.tile([P, SLOTS], U8, name=f"gs{s}", align_bytes=64) for s in range(PASSES)]
         w1 = [keep.tile([P, PASSES, 2 * H], U8, name=f"w1_{e}", align_bytes=64) for e in range(E)]
@@ -76,8 +77,9 @@ def tile_moe_cap2_glu_relu_kernel(
 
         for tile in (w3s, w1s, w2s):
             nc.vector.memset(tile[:].bitcast(I32), 0)
-        for s in range(PASSES):
-            nc.vector.memset(xs[s][:].bitcast(I32), 0)
+        nc.vector.memset(xs01[:].bitcast(I32), 0)
+        nc.vector.memset(xs2[:].bitcast(I32), 0)
+        nc.vector.memset(gs[0][:].bitcast(I32), 0)
         nc.gpsimd.memset(y[:, SLOTS:], 0.0)
         make_identity(nc, ident[:])
 
@@ -85,19 +87,10 @@ def tile_moe_cap2_glu_relu_kernel(
         nc.sync.dma_start(offs_t[:], offs)
         load_x(1)
         load_x(2)
+        load_w(0)
         load_scales(w1s, w1_scales, 0, 2)
         load_scales(w3s, w3_scales, 0, 2)
-        load_w(0)
         load_w(1)
-        load_w(2)
-        load_scales(w1s, w1_scales, 2, 4)
-        load_scales(w3s, w3_scales, 2, 4)
-        load_w(3)
-        load_scales(w2s, w2_scales, 0, 4)
-        nc.sync.dma_start(out=w2[:].bitcast(I32), in_=w2_words[:, 0].rearrange("e p n -> p e n").bitcast(I32))
-        nc.sync.dma_start(pos1_t[:], pos1)
-        nc.sync.dma_start(pos2_t[:], pos2)
-        nc.sync.dma_start(out=gates[:], in_=gate.rearrange("r p t -> p r t"))
 
         def prepare(s):
             for c in range(3):
@@ -110,7 +103,9 @@ def tile_moe_cap2_glu_relu_kernel(
             for start, stop in ((0, 512), (512, 768)):
                 cols = slice(start, stop)
                 nc.vector.quantize_mx(
-                    out=xw[s][:, cols].bitcast(FP8X4), scales=xs[s][:, cols], in_=xb[s][:, 4 * start : 4 * stop]
+                    out=xw[s][:, cols].bitcast(FP8X4),
+                    scales=(xs01[4:128, cols], xs01[:, cols], xs2[:, cols])[s],
+                    in_=xb[s][:, 4 * start : 4 * stop],
                 )
 
         def g_words(s, piece):
@@ -119,7 +114,13 @@ def tile_moe_cap2_glu_relu_kernel(
 
         def g_bytes(s, piece):
             start, stop = PIECE[piece]
-            nc.vector.tensor_copy(gs[s][:, start:stop], xs[s][:].indirect(offs_t[:, start // 16 : stop // 16]))
+            nc.vector.tensor_copy(gs[s][:, start:stop], (None, xs01, xs2)[s][:].indirect(offs_t[:, start // 16 : stop // 16]))
+            if s == 1:
+                for q in range(4):
+                    nc.sync.dma_start(
+                        out=gs[0][32 * q : 32 * q + 4, start:stop].bitcast(I32),
+                        in_=gs[1][32 * q + 4 : 32 * q + 8, start:stop].bitcast(I32),
+                    )
 
         acc, act, hid, hbf, codes = {}, {}, {}, {}, {}
 
@@ -139,8 +140,8 @@ def tile_moe_cap2_glu_relu_kernel(
                     lhsT_scale=gs[s][:, slots],
                     rhs=w[e][:, s, :].bitcast(FP4X4),
                     rhs_scale=ws[:, PASSES * e + s, :],
-                    start=(s == 0),
-                    stop=(s == PASSES - 1),
+                    start=(s == 1),
+                    stop=(s == 2),
                 )
 
         def relu(half):
@@ -167,65 +168,75 @@ def tile_moe_cap2_glu_relu_kernel(
                 nc.tensor.transpose(acc[half][0][:, cols], words[:, cols], ident[:])
 
         def tcp(half):
-            hbf[half] = stage.tile([P, 4 * 128], BF16, name="hb", align_bytes=64)
+            e, side = divmod(half, 2)
+            if side == 0:
+                hbf[e] = stage.tile([P, 4 * 256], BF16, name="hb", align_bytes=64)
             nc.scalar.copy(
-                hbf[half][:].bitcast(F32).rearrange("p (r u) -> p r u", u=2),
+                hbf[e][:, 512 * side : 512 * (side + 1)].bitcast(F32).rearrange("p (r u) -> p r u", u=2),
                 acc[half][0][:, 0:256].rearrange("p (u r) -> p r u", u=2),
             )
 
-        def hq(half):
-            hw = stage.tile([P, 128], U32, name="hw", align_bytes=64)
-            hs = stage.tile([P, 128], U8, name="hs", align_bytes=64)
-            nc.vector.quantize_mx(out=hw[:].bitcast(FP8X4), scales=hs[:], in_=hbf[half][:])
-            codes[half] = (hw, hs)
+        def hq(e, c0=0, c1=256):
+            if c0 == 0:
+                hw = stage.tile([P, 256], U32, name="hw", align_bytes=64)
+                hs = stage.tile([P, 256], U8, name="hs", align_bytes=64)
+                codes[e] = (hw, hs)
+            hw, hs = codes[e]
+            nc.vector.quantize_mx(out=hw[:, c0:c1].bitcast(FP8X4), scales=hs[:, c0:c1], in_=hbf[e][:, 4 * c0 : 4 * c1])
 
-        def m2(half):
-            e = half // 2
-            hw, hs = codes[half]
+        def m2(e, c0=0, c1=256):
+            hw, hs = codes[e]
+            bank = acc[2 * e + 1 if c1 == 256 else 2 * e][0]
             nc.tensor.matmul_mx(
-                out=acc[half][0][:, 256:384],
+                out=bank[:, 256 : 256 + c1 - c0],
                 lhsT=w2[:, e, :].bitcast(FP4X4),
                 lhsT_scale=w2s[:, e, :],
-                rhs=hw[:].bitcast(FP8X4),
-                rhs_scale=hs[:],
+                rhs=hw[:, c0:c1].bitcast(FP8X4),
+                rhs_scale=hs[:, c0:c1],
                 start=True,
                 stop=True,
             )
 
-        def ycp(half):
-            nc.scalar.copy(y[:, 128 * half : 128 * (half + 1)], acc[half][0][:, 256:384])
+        def ycp(e, c0=0, c1=256):
+            bank = acc[2 * e + 1 if c1 == 256 else 2 * e][0]
+            nc.scalar.copy(y[:, 256 * e + c0 : 256 * e + c1], bank[:, 256 : 256 + c1 - c0])
 
-        prepare(0); g_words(0, "F"); g_bytes(0, "F"); g_bytes(0, "C")
-        prepare(1); g_words(1, "F"); g_bytes(1, "F")
-        prepare(2); g_bytes(2, "A"); g_words(2, "A"); g_words(0, "C"); g_words(2, "B"); g_bytes(2, "B")
-        for h in (0, 1):
-            mm(h, 0); mm(h, 1)
+        A, B = (0,), (1,)
+        prepare(0); g_words(0, "F"); g_words(0, "C")
+        prepare(1); g_bytes(1, "F"); g_words(1, "F"); g_bytes(1, "C")
+        load_scales(w1s, w1_scales, 2, 4)
+        load_scales(w3s, w3_scales, 2, 4)
+        load_w(2)
+        load_scales(w2s, w2_scales, 0, 4)
+        nc.sync.dma_start(out=w2[:].bitcast(I32), in_=w2_words[:, 0].rearrange("e p n -> p e n").bitcast(I32))
+        load_w(3)
+        nc.sync.dma_start(pos1_t[:], pos1)
+        nc.sync.dma_start(pos2_t[:], pos2)
+        nc.sync.dma_start(out=gates[:], in_=gate.rearrange("r p t -> p r t"))
+
+        prepare(2); g_bytes(2, "A"); g_words(2, "A"); g_bytes(2, "B"); g_words(1, "C"); g_words(2, "B")
+        mm(0, 1, A); mm(1, 1, A); mm(0, 1, B); mm(1, 1, B); mm(0, 0); mm(1, 0)
         for h in (0, 1):
             mm(h, 2); relu(h)
         for h in (2, 3):
-            mm(h, 0); mm(h, 1)
+            mm(h, 1); mm(h, 0)
         for h in (2, 3):
             mm(h, 2); relu(h)
-        g_words(1, "C"); mul(0); mul(1); g_bytes(1, "C"); mul(2); mul(3)
-        tr(0); tr(1); tcp(0); tcp(1); mm(4, 0); hq(0); hq(1)
-        g_words(2, "C"); g_bytes(2, "C")
-        mm(4, 1); tr(2); tr(3); tcp(2); tcp(3); m2(0); m2(1); ycp(0); ycp(1); mm(5, 0); mm(5, 1)
-        hq(2); hq(3)
-        m2(2); m2(3); ycp(2); ycp(3); mm(6, 0); mm(4, 2); relu(4); mm(5, 2); relu(5)
-        mm(6, 1); mm(6, 2); relu(6); mm(7, 0); mul(4); mul(5)
-        mm(7, 1); tr(4); tr(5); tcp(4); tcp(5); mm(7, 2, (0,)); relu(7); mm(7, 2, (1,)); mul(6); hq(4); hq(5); mul(7)
-        tr(6); m2(4); m2(5); tr(7); tcp(6); ycp(4); ycp(5); tcp(7); hq(6); hq(7); m2(6); ycp(6); m2(7); ycp(7)
+        mul(0); g_words(2, "C"); mul(1); g_bytes(2, "C"); mul(2); mul(3)
+        mm(4, 1, A); mm(4, 0, A); tr(0); tr(1); tcp(0); mm(4, 1, B); mm(4, 0, B); tcp(1); hq(0)
+        mm(4, 2); relu(4); mm(5, 1, A); mm(5, 0, A); tr(2); tr(3); tcp(2); tcp(3); m2(0); ycp(0); hq(1)
+        mm(5, 1, B); mm(5, 0, B); mm(5, 2); relu(5); mul(4)
+        mm(6, 1); mm(6, 0); m2(1); ycp(1); mul(5); mm(6, 2); relu(6)
+        mm(7, 1, A); mm(7, 0, A); mm(7, 2, A); relu(7); mm(7, 1, B); mm(7, 0, B); mm(7, 2, B); mul(6); mul(7)
+        tr(4); tr(5); tcp(4); tcp(5); tr(6); tcp(6); tr(7); hq(2); hq(3, 0, 128); tcp(7); hq(3, 128, 256)
+        m2(2); m2(3, 0, 128); ycp(2); ycp(3, 0, 128); m2(3, 128, 256); ycp(3, 128, 256)
 
-        parts = []
+        t1 = keep.tile([P, T], F32, name="t1")
+        t2 = keep.tile([P, T], F32, name="t2")
+        o = keep.tile([P, T], F32, name="o")
+        nc.vector.tensor_tensor(t1[:], y[:].indirect(pos1_t[:]), gates[:, 0, :], MULT)
+        nc.vector.tensor_tensor(t2[:], y[:].indirect(pos2_t[:]), gates[:, 1, :], MULT)
         for c in range(2):
             cols = slice(384 * c, 384 * (c + 1))
-            idx = slice(24 * c, 24 * (c + 1))
-            t1 = stage.tile([P, 384], F32, name="t1")
-            t2 = stage.tile([P, 384], F32, name="t2")
-            nc.vector.tensor_tensor(t1[:], y[:].indirect(pos1_t[:, idx]), gates[:, 0, cols], MULT)
-            nc.vector.tensor_tensor(t2[:], y[:].indirect(pos2_t[:, idx]), gates[:, 1, cols], MULT)
-            parts.append((cols, t1, t2))
-        for cols, t1, t2 in parts:
-            o = stage.tile([P, 384], F32, name="o")
-            nc.vector.tensor_tensor(o[:], t1[:], t2[:], ADD)
-            nc.sync.dma_start(out=out[:, cols], in_=o[:])
+            nc.vector.tensor_tensor(o[:, cols], t1[:, cols], t2[:, cols], ADD)
+            nc.sync.dma_start(out=out[:, cols], in_=o[:, cols])

@@ -60,7 +60,8 @@ def tile_moe_cap2_glu_relu_kernel(
 
         def load_x(s):
             rows = xT[512 * s : 512 * (s + 1), :].rearrange("(p j) t -> p j t", j=4)
-            nc.sync.dma_start(out=xf[s][:], in_=rows)
+            for cols in (slice(0, 512), slice(512, 768)) if s == 0 else (slice(0, 768),):
+                nc.sync.dma_start(out=xf[s][:, :, cols], in_=rows[:, :, cols])
 
         def load_w(e):
             for tile, dram in ((w1[e], w1_words), (w3[e], w3_words)):

from contextlib import ExitStack

import concourse.mybir as mybir
from concourse.masks import make_identity

K, T, E, C, H, N = 1536, 768, 4, 256, 512, 128
PAD = 32
FLOPS = 3355443200

F32 = mybir.dt.float32
BF16 = mybir.dt.bfloat16
U32 = mybir.dt.uint32
I32 = mybir.dt.int32
U16 = mybir.dt.uint16
U8 = mybir.dt.uint8
FP8X4 = mybir.dt.float8_e4m3fn_x4
FP4X4 = mybir.dt.float4_e2m1fn_x4
COPY = mybir.ActivationFunctionType.Copy
RELU = mybir.ActivationFunctionType.Relu
MULT = mybir.AluOpType.mult
ADD = mybir.AluOpType.add

P = 128
PASSES = K // 512
SLOTS = E * C
CHUNK = 256
VECTOR_CHUNKS = {(0, 0), (0, 2), (1, 1)}
BANKS = ((0, 1), (2, 3), (4, 5), (6, 7), (1, 3), (5, 7), (0, 2), (4, 6))
PIECE = {"A": (0, 256), "B": (256, 512), "F": (0, 512), "C": (512, 1024)}


def tile_moe_cap2_glu_relu_kernel(
    tc, xT, w1_words, w1_scales, w3_words, w3_scales, w2_words, w2_scales, gate, offs, pos1, pos2, out
):
    nc = tc.nc
    with ExitStack() as ctx:
        keep = ctx.enter_context(tc.tile_pool(name="keep", bufs=1))
        stage = ctx.enter_context(tc.tile_pool(name="stage", bufs=4))
        psum = ctx.enter_context(tc.psum_pool(name="psum", bufs=1))

        offs_t = keep.tile([P, SLOTS // 16], U16, name="offs_t")
        pos1_t = keep.tile([P, T // 16], U16, name="pos1_t")
        pos2_t = keep.tile([P, T // 16], U16, name="pos2_t")
        xf = [keep.tile([P, 4, T], F32, name=f"xf{s}") for s in range(PASSES)]
        xb = [keep.tile([P, 4 * T], BF16, name=f"xb{s}", align_bytes=64) for s in range(PASSES)]
        xw = [keep.tile([P, T], U32, name=f"xw{s}", align_bytes=64) for s in range(PASSES)]
        xs01 = keep.tile([P, T], U8, name="xs01", align_bytes=64)
        xs2 = keep.tile([P, T], U8, name="xs2", align_bytes=64)
        gw = [keep.tile([P, SLOTS], U32, name=f"gw{s}", align_bytes=64) for s in range(PASSES)]
        gs = [keep.tile([P, SLOTS], U8, name=f"gs{s}", align_bytes=64) for s in range(PASSES)]
        w1 = [keep.tile([P, PASSES, 2 * H], U8, name=f"w1_{e}", align_bytes=64) for e in range(E)]
        w3 = [keep.tile([P, PASSES, 2 * H], U8, name=f"w3_{e}", align_bytes=64) for e in range(E)]
        w2 = keep.tile([P, E, 2 * N], U8, name="w2", align_bytes=64)
        w1s = keep.tile([P, E * PASSES, H], U8, name="w1s", align_bytes=64)
        w3s = keep.tile([P, E * PASSES, H], U8, name="w3s", align_bytes=64)
        w2s = keep.tile([P, E, N], U8, name="w2s", align_bytes=64)
        gates = keep.tile([P, 2, T], F32, name="gates")
        y = keep.tile([P, SLOTS + PAD], F32, name="y")
        ident = keep.tile([P, P], F32, name="ident")

        def load_x(s):
            rows = xT[512 * s : 512 * (s + 1), :].rearrange("(p j) t -> p j t", j=4)
            for cols in (slice(0, 512), slice(512, 768)) if s == 0 else (slice(0, 768),):
                nc.sync.dma_start(out=xf[s][:, :, cols], in_=rows[:, :, cols])

        def load_w(e):
            for tile, dram in ((w1[e], w1_words), (w3[e], w3_words)):
                nc.sync.dma_start(out=tile[:].bitcast(I32), in_=dram[e].rearrange("s p n -> p s n").bitcast(I32))

        def load_scales(tile, dram, e0, e1):
            passes = dram.shape[1]
            rows = dram[e0:e1].rearrange("e s q n -> q (e s) n")
            for quad in range(4):
                nc.sync.dma_start(
                    out=tile[32 * quad : 32 * quad + 4, passes * e0 : passes * e1, :].bitcast(I32),
                    in_=rows[4 * quad : 4 * quad + 4, :, :].bitcast(I32),
                )

        for tile in (w3s, w1s, w2s):
            nc.vector.memset(tile[:].bitcast(I32), 0)
        nc.vector.memset(xs01[:].bitcast(I32), 0)
        nc.vector.memset(xs2[:].bitcast(I32), 0)
        nc.vector.memset(gs[0][:].bitcast(I32), 0)
        nc.gpsimd.memset(y[:, SLOTS:], 0.0)
        make_identity(nc, ident[:])

        load_x(0)
        nc.sync.dma_start(offs_t[:], offs)
        load_x(1)
        load_x(2)
        load_w(0)
        load_scales(w1s, w1_scales, 0, 2)
        load_scales(w3s, w3_scales, 0, 2)
        load_w(1)

        def prepare(s):
            for c in range(3):
                dst = xb[s][:, 4 * CHUNK * c : 4 * CHUNK * (c + 1)].rearrange("p (c i j) -> p c j i", i=4, j=4)
                src = xf[s][:, :, CHUNK * c : CHUNK * (c + 1)].rearrange("p j (c i) -> p c j i", i=4)
                if (s, c) in VECTOR_CHUNKS:
                    nc.vector.tensor_copy(dst, src)
                else:
                    nc.scalar.activation(dst, src, COPY)
            for start, stop in ((0, 512), (512, 768)):
                cols = slice(start, stop)
                nc.vector.quantize_mx(
                    out=xw[s][:, cols].bitcast(FP8X4),
                    scales=(xs01[4:128, cols], xs01[:, cols], xs2[:, cols])[s],
                    in_=xb[s][:, 4 * start : 4 * stop],
                )

        def g_words(s, piece):
            start, stop = PIECE[piece]
            nc.vector.tensor_copy(gw[s][:, start:stop], xw[s][:].indirect(offs_t[:, start // 16 : stop // 16]))

        def g_bytes(s, piece):
            start, stop = PIECE[piece]
            nc.vector.tensor_copy(gs[s][:, start:stop], (None, xs01, xs2)[s][:].indirect(offs_t[:, start // 16 : stop // 16]))
            if s == 1:
                for q in range(4):
                    nc.sync.dma_start(
                        out=gs[0][32 * q : 32 * q + 4, start:stop].bitcast(I32),
                        in_=gs[1][32 * q + 4 : 32 * q + 8, start:stop].bitcast(I32),
                    )

        acc, act, hid, hbf, codes = {}, {}, {}, {}, {}

        def open_banks(half):
            acc[half] = [psum.tile([P, H], F32, name=f"bank{b}") for b in BANKS[half]]

        def mm(half, s, which=(0, 1)):
            if half not in acc:
                open_banks(half)
            e = half // 2
            slots = slice(128 * half, 128 * (half + 1))
            for m in which:
                w, ws = ((w1, w1s), (w3, w3s))[m]
                nc.tensor.matmul_mx(
                    out=acc[half][m][:],
                    lhsT=gw[s][:, slots].bitcast(FP8X4),
                    lhsT_scale=gs[s][:, slots],
                    rhs=w[e][:, s, :].bitcast(FP4X4),
                    rhs_scale=ws[:, PASSES * e + s, :],
                    start=(s == 1),
                    stop=(s == 2),
                )

        def relu(half):
            act[half] = stage.tile([P, H], F32, name="ra")
            nc.scalar.activation(
                act[half][:].rearrange("m (u p d) -> m u p d", u=2, d=2),
                acc[half][0][:].rearrange("m (p u d) -> m u p d", u=2, d=2),
                RELU,
            )

        def mul(half):
            hid[half] = stage.tile([P, H], BF16, name="h", align_bytes=64)
            nc.vector.tensor_tensor(
                hid[half][:].rearrange("m (u p d) -> m u p d", u=2, d=2),
                acc[half][1][:].rearrange("m (p u d) -> m u p d", u=2, d=2),
                act[half][:].rearrange("m (u p d) -> m u p d", u=2, d=2),
                MULT,
            )

        def tr(half):
            words = hid[half][:].bitcast(F32)
            for u in range(2):
                cols = slice(128 * u, 128 * (u + 1))
                nc.tensor.transpose(acc[half][0][:, cols], words[:, cols], ident[:])

        def tcp(half):
            e, side = divmod(half, 2)
            if side == 0:
                hbf[e] = stage.tile([P, 4 * 256], BF16, name="hb", align_bytes=64)
            nc.scalar.copy(
                hbf[e][:, 512 * side : 512 * (side + 1)].bitcast(F32).rearrange("p (r u) -> p r u", u=2),
                acc[half][0][:, 0:256].rearrange("p (u r) -> p r u", u=2),
            )

        def hq(e, c0=0, c1=256):
            if c0 == 0:
                hw = stage.tile([P, 256], U32, name="hw", align_bytes=64)
                hs = stage.tile([P, 256], U8, name="hs", align_bytes=64)
                codes[e] = (hw, hs)
            hw, hs = codes[e]
            nc.vector.quantize_mx(out=hw[:, c0:c1].bitcast(FP8X4), scales=hs[:, c0:c1], in_=hbf[e][:, 4 * c0 : 4 * c1])

        def m2(e, c0=0, c1=256):
            hw, hs = codes[e]
            bank = acc[2 * e + 1 if c1 == 256 else 2 * e][0]
            nc.tensor.matmul_mx(
                out=bank[:, 256 : 256 + c1 - c0],
                lhsT=w2[:, e, :].bitcast(FP4X4),
                lhsT_scale=w2s[:, e, :],
                rhs=hw[:, c0:c1].bitcast(FP8X4),
                rhs_scale=hs[:, c0:c1],
                start=True,
                stop=True,
            )

        def ycp(e, c0=0, c1=256):
            bank = acc[2 * e + 1 if c1 == 256 else 2 * e][0]
            nc.scalar.copy(y[:, 256 * e + c0 : 256 * e + c1], bank[:, 256 : 256 + c1 - c0])

        A, B = (0,), (1,)
        prepare(0); g_words(0, "F"); g_words(0, "C")
        prepare(1); g_bytes(1, "F"); g_words(1, "F"); g_bytes(1, "C")
        load_scales(w1s, w1_scales, 2, 4)
        load_scales(w3s, w3_scales, 2, 4)
        load_w(2)
        load_scales(w2s, w2_scales, 0, 4)
        nc.sync.dma_start(out=w2[:].bitcast(I32), in_=w2_words[:, 0].rearrange("e p n -> p e n").bitcast(I32))
        load_w(3)
        nc.sync.dma_start(pos1_t[:], pos1)
        nc.sync.dma_start(pos2_t[:], pos2)
        nc.sync.dma_start(out=gates[:], in_=gate.rearrange("r p t -> p r t"))

        prepare(2); g_bytes(2, "A"); g_words(2, "A"); g_bytes(2, "B"); g_words(1, "C"); g_words(2, "B")
        mm(0, 1, A); mm(1, 1, A); mm(0, 1, B); mm(1, 1, B); mm(0, 0); mm(1, 0)
        for h in (0, 1):
            mm(h, 2); relu(h)
        for h in (2, 3):
            mm(h, 1); mm(h, 0)
        for h in (2, 3):
            mm(h, 2); relu(h)
        mul(0); g_words(2, "C"); mul(1); g_bytes(2, "C"); mul(2); mul(3)
        mm(4, 1, A); mm(4, 0, A); tr(0); tr(1); tcp(0); mm(4, 1, B); mm(4, 0, B); tcp(1); hq(0)
        mm(4, 2); relu(4); mm(5, 1, A); mm(5, 0, A); tr(2); tr(3); tcp(2); tcp(3); m2(0); ycp(0); hq(1)
        mm(5, 1, B); mm(5, 0, B); mm(5, 2); relu(5); mul(4)
        mm(6, 1); mm(6, 0); m2(1); ycp(1); mul(5); mm(6, 2); relu(6)
        mm(7, 1, A); mm(7, 0, A); mm(7, 2, A); relu(7); mm(7, 1, B); mm(7, 0, B); mm(7, 2, B); mul(6); mul(7)
        tr(4); tr(5); tcp(4); tcp(5); tr(6); tcp(6); tr(7); hq(2); hq(3, 0, 128); tcp(7); hq(3, 128, 256)
        m2(2); m2(3, 0, 128); ycp(2); ycp(3, 0, 128); m2(3, 128, 256); ycp(3, 128, 256)

        t1 = keep.tile([P, T], F32, name="t1")
        t2 = keep.tile([P, T], F32, name="t2")
        o = keep.tile([P, T], F32, name="o")
        nc.vector.tensor_tensor(t1[:], y[:].indirect(pos1_t[:]), gates[:, 0, :], MULT)
        nc.vector.tensor_tensor(t2[:], y[:].indirect(pos2_t[:]), gates[:, 1, :], MULT)
        for c in range(2):
            cols = slice(384 * c, 384 * (c + 1))
            nc.vector.tensor_tensor(o[:, cols], t1[:, cols], t2[:, cols], ADD)
            nc.sync.dma_start(out=out[:, cols], in_=o[:, cols])
